import numpy as np
import ml_dtypes


def mxq(x, axis, fmt="e4m3"):
    dtype, down = {"e4m3": (ml_dtypes.float8_e4m3fn, 7), "e5m2": (ml_dtypes.float8_e5m2, 14)}[fmt]
    v = np.moveaxis(np.asarray(x, np.float32).astype(ml_dtypes.bfloat16).astype(np.float64), axis, -1)
    blocks = v.reshape(v.shape[:-1] + (-1, 32))
    amax = np.abs(blocks).max(-1, keepdims=True)
    byte = np.maximum(np.where(amax > 0, np.frexp(amax)[1] - 1 + 127, 0) - down, 1)
    scale = np.exp2(byte - 127.0)
    codes = (blocks / scale).astype(np.float32).astype(dtype).astype(np.float64)
    return np.moveaxis((codes * scale).reshape(v.shape), -1, axis)


WIDE = False


def mx_kscale(k):
    if not WIDE:
        return np.ones(k)
    levels = np.array([10, -10, 5, -5, 0])
    if k % 512:
        return np.exp2(np.random.permutation(np.resize(levels, k // 32))).repeat(32)
    a = np.empty((k // 512, 16))
    for p in range(k // 512):
        a[p, :8] = np.random.permutation(np.resize(levels, 8))
        for g in range(8):
            far = levels[np.abs(levels - a[p, g]) >= 10]
            a[p, g + 8] = far[np.random.randint(len(far))]
    return np.exp2(a.ravel()).repeat(32)


BF16 = ml_dtypes.bfloat16


def bf(x):
    return np.asarray(x, np.float32).astype(BF16)


def f64(x):
    return np.asarray(x).astype(np.float64)


E2M1 = np.array([0.0, 0.5, 1.0, 1.5, 2.0, 3.0, 4.0, 6.0, -0.0, -0.5, -1.0, -1.5, -2.0, -3.0, -4.0, -6.0])


def pack_weight(w, fmt):
    k, n = w.shape
    w = f64(bf(w)).reshape(k // 32, 32, n)
    amax = np.abs(w).max(1)
    if fmt == "e4m3":
        byte = np.frexp(amax)[1] - 1 + 127 - 7
    else:
        mant, ex = np.frexp(amax / 6.0)
        byte = np.where(mant > 0.5, ex, ex - 1) + 127
    byte = np.clip(np.where(amax > 0, byte, 1), 1, 254)
    scaled = (w * np.exp2(127.0 - byte)[:, None, :]).reshape(k, n).astype(np.float32)
    by_word = np.ascontiguousarray(scaled.reshape(k // 512, 128, 4, n).transpose(0, 1, 3, 2))
    if fmt == "e4m3":
        words = by_word.astype(ml_dtypes.float8_e4m3fn).view(np.uint8)
    else:
        c = by_word.astype(ml_dtypes.float4_e2m1fn).view(np.uint8) & 0xF
        words = c[..., 0::2] | (c[..., 1::2] << 4)
    return np.ascontiguousarray(words), np.ascontiguousarray(byte.astype(np.uint8).reshape(k // 512, 16, n))


def unpack_weight(words, scales, fmt):
    g, p, n, _ = words.shape
    if fmt == "e4m3":
        vals = np.ascontiguousarray(words).view(ml_dtypes.float8_e4m3fn).astype(np.float64)
    else:
        nib = np.empty((g, p, n, 4), np.uint8)
        nib[..., 0::2] = words & 0xF
        nib[..., 1::2] = words >> 4
        vals = E2M1[nib]
    vals = vals * np.repeat(np.exp2(scales.astype(np.float64) - 127.0), 8, axis=1)[..., None]
    return vals.transpose(0, 1, 3, 2).reshape(g * 512, n)

E4M3FN = np.array([(-1.0 if i & 128 else 1.0) * ((1.0 + (i & 7) / 8.0) * 2.0 ** (((i >> 3) & 15) - 7) if i & 120 else (i & 7) * 2.0 ** -9) for i in range(256)])


def e4m3fn_bytes(y):
    return np.clip(np.asarray(y, np.float64), -448.0, 448.0).astype(np.float32).astype(ml_dtypes.float8_e4m3fn).view(np.uint8)


def e4m3fn_values(b):
    return E4M3FN[b]


T, D, F, R = 1024, 1024, 1024, 512


def hadamard_delta(p1, p2):
    return 0.05 * np.tanh(p1) * (1.0 + np.tanh(p2))


def draw0():
    s = mx_kscale(D)
    a, b = mx_kscale(R), mx_kscale(R)
    x = bf(np.random.standard_normal((T, D)) / s[None, :])
    w0 = bf(np.random.standard_normal((D, F)) / np.sqrt(D))
    x1_words, x1_scales = pack_weight((np.random.standard_normal((D, R)) * a[None, :]).T, "e4m3")
    y1_words, y1_scales = pack_weight(np.random.standard_normal((R, F)) / np.sqrt(R) / a[:, None], "e4m3")
    x2_words, x2_scales = pack_weight((np.random.standard_normal((D, R)) * b[None, :]).T, "e4m3")
    y2_words, y2_scales = pack_weight(np.random.standard_normal((R, F)) / np.sqrt(R) / b[:, None], "e4m3")
    return {
        "x": x,
        "w0": w0,
        "x1_words": x1_words,
        "x1_scales": x1_scales,
        "y1_words": y1_words,
        "y1_scales": y1_scales,
        "x2_words": x2_words,
        "x2_scales": x2_scales,
        "y2_words": y2_words,
        "y2_scales": y2_scales,
        "gain": bf((1.0 + 0.1 * np.random.standard_normal(D)) * s),
    }


def core(x, w0, x1_words, x1_scales, y1_words, y1_scales, x2_words, x2_scales, y2_words, y2_scales, gain):
    p1 = unpack_weight(x1_words, x1_scales, "e4m3").T @ unpack_weight(y1_words, y1_scales, "e4m3")
    p2 = unpack_weight(x2_words, x2_scales, "e4m3").T @ unpack_weight(y2_words, y2_scales, "e4m3")
    dw = hadamard_delta(p1, p2)
    w = f64(gain)[:, None] * (f64(w0) + dw)
    return mxq(f64(x), 1, "e4m3") @ mxq(w, 0, "e4m3")


def setup_inputs():
    drawn = draw0()
    full = np.asarray(drawn['x']).astype(np.float64)
    scale = (np.abs(full).reshape(1024, 8, 128).max(axis=(2,)) / 448.0).astype(np.float32)
    given = {}
    for key, value in drawn.items():
        if key == 'x':
            given['x_bytes'] = e4m3fn_bytes(full / np.repeat(scale.astype(np.float64), 128, axis=1))
            given['x_scale'] = scale
        else:
            given[key] = value
    return given


def reference(x_bytes, x_scale, w0, x1_words, x1_scales, y1_words, y1_scales, x2_words, x2_scales, y2_words, y2_scales, gain):
    return core(e4m3fn_values(x_bytes) * np.repeat(x_scale.astype(np.float64), 128, axis=1), w0, x1_words, x1_scales, y1_words, y1_scales, x2_words, x2_scales, y2_words, y2_scales, gain)

@@ -1,0 +1,340 @@
+from contextlib import ExitStack
+
+import concourse.mybir as mybir
+from concourse.masks import make_identity
+
+T, D, F, R = 1024, 1024, 1024, 512
+P = 128
+FLOPS = 2 * D * F * R * 2 + 2 * T * D * F
+
+F32 = mybir.dt.float32
+BF16 = mybir.dt.bfloat16
+I32 = mybir.dt.int32
+U8 = mybir.dt.uint8
+FP8 = mybir.dt.float8_e4m3fn
+FP8X4 = mybir.dt.float8_e4m3fn_x4
+ACT = mybir.ActivationFunctionType
+ALU = mybir.AluOpType
+
+NT = T // P
+WIDTHS = (256, 256, 256, 128, 128)
+STARTS = (0, 256, 512, 768, 896)
+NC = len(WIDTHS)
+NU = 2 * NC
+S_WIDEN = (1,)
+ORDER = (
+    "G0 P0 D0 W0 T0 W2 W1 O0 T1 W3 P1 O1 Q0 T2 Q1 O2 T3 O3 W4 Q2 T4 P2 O4 M0 "
+    "W5 A0 P3 P4 T5 P5 O5 M1 Q3 A1 P6 Q4 M2 M3 A2 W6 M4 A3 T6 W7 P7 A4 M5 A5 "
+    "B0 M6 M7 H0 A6 Q5 B1 A7 M8 C0 M9 A8 M10 M11 A9 H1 B2 A10 M12 C1 M13 O6 C2 A11 "
+    "B3 M14 C3 A12 B4 A13 T7 A14 M15 H2 M16 K0 O7 B5 Q6 M17 A15 C4 M18 A16 K1 A17 X0 M19 "
+    "E0 H3 M20 C5 A18 B6 C6 A19 X1 M21 A20 Q7 X2 E1 B7 B8 A21 M22 H4 M23 C7 A22 M24 K2 "
+    "E2 X3 C8 B9 E3 M25 K3 A23 X4 A24 M26 H5 E4 B10 C9 A25 X5 C10 M27 E5 X6 A26 B11 H6 "
+    "C11 M28 A27 M29 K4 B12 A28 K5 B13 C12 E6 X7 A29 M30 H7 X8 E7 M31 A30 H8 C13 X9 E8 B14 "
+    "E9 C14 X10 A31 K6 K7 E10 X11 B15 E11 H9 K8 C15 X12 E12 K9 X13 E13 X14 E14 X15 V15 "
+).split()
+
+
+def tile_fedparatanhhadamardlinear_d1p_kernel(
+    tc, x_bytes, x_scale, w0, x1_words, x1_scales, y1_words, y1_scales,
+    x2_words, x2_scales, y2_words, y2_scales, gain, out,
+):
+    nc = tc.nc
+    with ExitStack() as ctx:
+        ctx.enter_context(tc.manual_schedule())
+        keep = ctx.enter_context(tc.tile_pool(name="keep", bufs=1))
+        work = ctx.enter_context(tc.tile_pool(name="work", bufs=3))
+        psum = ctx.enter_context(tc.psum_pool(name="psum", bufs=2))
+
+        x_v = x_bytes.rearrange("(p i) k -> p i k", i=NT)
+        out_v = out.rearrange("(p i) f -> p i f", i=NT)
+        w0_v = w0.rearrange("(g p t) f -> g p t f", g=2, t=4)
+
+        def words_of(ap):
+            return ap[0].rearrange("p n t -> p (n t)").bitcast(I32)
+
+        ident = keep.tile([P, P], F32, name="ident", align_bytes=64)
+        warm = keep.tile([P, 1], F32, name="warm")
+        scale_raw = {}
+        for nm in ("x1", "y1", "x2", "y2"):
+            scale_raw[nm] = keep.tile([P, 1024], U8, name="sraw_" + nm, align_bytes=64)
+        nc.vector.memset(warm[:], 0.0)
+        for nm in ("x1", "y1", "x2", "y2"):
+            nc.vector.memset(scale_raw[nm][:].bitcast(I32), 0)
+
+        def load_scales(nm, ap, eng):
+            src = ap[0].bitcast(I32)
+            for q in range(4):
+                eng.dma_start(out=scale_raw[nm][32 * q : 32 * q + 4, :].bitcast(I32), in_=src[4 * q : 4 * q + 4, :])
+
+        xs = keep.tile([P, NT * 8], F32, name="xs")
+        xb = [keep.tile([P, 2, 1024], U8, name=f"xb{h}", align_bytes=64) for h in range(4)]
+        w0t = [keep.tile([P, 4, F], BF16, name=f"w0t{g}", align_bytes=64) for g in range(2)]
+        xraw = {(nm, g): keep.tile([P, 512], I32, name=f"xraw{nm}{g}", align_bytes=64) for nm in ("x1", "x2") for g in range(2)}
+        yw = {nm: keep.tile([P, 1024], I32, name="yw" + nm, align_bytes=64) for nm in ("y1", "y2")}
+        gain_b = keep.tile([P, 2, 4], BF16, name="gain_b")
+
+        def load_xb(h):
+            nc.sync.dma_start(out=xb[h][:], in_=x_v[:, 2 * h : 2 * h + 2, :])
+
+        def load_xw(nm, ap, g, eng=nc.sync):
+            eng.dma_start(out=xraw[nm, g][:], in_=words_of(ap)[:, 512 * g : 512 * (g + 1)])
+
+        def load_y(nm, ap, f0, f1, eng=nc.sync):
+            eng.dma_start(out=yw[nm][:, f0:f1], in_=words_of(ap)[:, f0:f1])
+
+        def load_w0(g, h):
+            nc.sync.dma_start(out=w0t[g][:, :, 512 * h : 512 * (h + 1)], in_=w0_v[g][:, :, 512 * h : 512 * (h + 1)])
+
+        nc.sync.dma_start(out=gain_b[:], in_=gain.rearrange("(g p t) -> p g t", g=2, t=4))
+        nc.sync.dma_start(out=xs[:], in_=x_scale.rearrange("(p i) j -> p (i j)", i=NT))
+        load_scales("x1", x1_scales, nc.sync)
+        load_xb(0)
+        load_xb(1)
+        load_scales("y1", y1_scales, nc.sync)
+        load_y("y1", y1_words, 0, 256, nc.sync)
+        load_xb(2)
+        load_xw("x1", x1_words, 0, nc.sync)
+        load_xw("x1", x1_words, 1, nc.sync)
+        load_scales("x2", x2_scales, nc.sync)
+        load_y("y2", y2_words, 0, 256, nc.sync)
+        load_xw("x2", x2_words, 0, nc.sync)
+        load_xb(3)
+        load_scales("y2", y2_scales, nc.sync)
+        load_xw("x2", x2_words, 1, nc.sync)
+        load_w0(0, 0)
+        load_y("y1", y1_words, 256, F, nc.sync)
+        load_y("y2", y2_words, 256, F, nc.sync)
+        load_w0(1, 0)
+        load_w0(0, 1)
+        load_w0(1, 1)
+
+        make_identity(nc, ident[:])
+        nc.scalar.activation(out=warm[:], in_=warm[:], func=ACT.Sigmoid)
+
+        xw, xbank, xg, xc, xsc = {}, {}, {}, {}, {}
+
+        def x_widen(i):
+            xw[i] = work.tile([P, 1024], BF16, name="xw", align_bytes=64)
+            for j in range(8):
+                dst = xw[i][:, 128 * j : 128 * (j + 1)]
+                src = xb[i // 2][:, i % 2, 128 * j : 128 * (j + 1)].bitcast(FP8)
+                scale = xs[:, 8 * i + j : 8 * i + j + 1]
+                if i in S_WIDEN:
+                    nc.scalar.activation(out=dst, in_=src, func=ACT.Copy, scale=scale)
+                else:
+                    nc.vector.tensor_scalar(out=dst, in0=src, scalar1=scale, scalar2=None, op0=ALU.mult)
+
+        def x_turn(i):
+            xbank[i] = psum.tile([P, 4, P], F32, name="ob")
+            words = xw[i][:].bitcast(F32)
+            for g in range(2):
+                for u in range(2):
+                    nc.tensor.transpose(xbank[i][:, 2 * g + u, :], words[:, 256 * g + u : 256 * (g + 1) : 2], ident[:])
+
+        def x_out(i):
+            xg[i] = work.tile([P, 1024], BF16, name="xg", align_bytes=64)
+            nc.scalar.copy(
+                out=xg[i][:].bitcast(F32).rearrange("p (g r u) -> p g r u", g=2, u=2),
+                in_=xbank[i][:].rearrange("p (g u) r -> p g r u", g=2),
+            )
+
+        def x_quant(i):
+            xc[i] = keep.tile([P, 2, P], I32, name=f"xc{i}", align_bytes=64)
+            xsc[i] = keep.tile([P, 2, P], U8, name=f"xsc{i}", align_bytes=64)
+            nc.vector.quantize_mx(
+                out=xc[i][:].rearrange("p g r -> p (g r)").bitcast(FP8X4),
+                scales=xsc[i][:].rearrange("p g r -> p (g r)"),
+                in_=xg[i][:],
+            )
+
+        xp, xps = {}, {}
+
+        def order_words(nm, g):
+            xp[nm, g] = keep.tile([P, 4, P], I32, name=f"xp{nm}{g}", align_bytes=64)
+            nc.vector.tensor_copy(out=xp[nm, g][:], in_=xraw[nm, g][:].rearrange("p (m t) -> p t m", t=4))
+
+        def order_scales(nm, g):
+            xps[nm, g] = keep.tile([P, 4, P], U8, name=f"xps{nm}{g}", align_bytes=64)
+            nc.vector.tensor_copy(
+                out=xps[nm, g][:],
+                in_=scale_raw[nm][:, 512 * g : 512 * (g + 1)].rearrange("p (m t) -> p t m", t=4),
+            )
+
+        def unit(j):
+            return j // 2, j % 2
+
+        acts, pbank = {}, {}
+
+        def product(j, which, h):
+            c, g = unit(j)
+            w, f0 = WIDTHS[c], STARTS[c]
+            n = 512 // w
+            nx, ny = (("x1", "y1"), ("x2", "y2"))[which]
+            bank = psum.tile([P, n, w], F32, name="pb", bufs=4)
+            pbank[j, which, h] = bank
+            for k in range(n):
+                t = n * h + k
+                nc.tensor.matmul_mx(
+                    out=bank[:, k, :],
+                    lhsT=xp[nx, g][:, t, :].bitcast(FP8X4),
+                    lhsT_scale=xps[nx, g][:, t, :],
+                    rhs=yw[ny][:, f0 : f0 + w].bitcast(FP8X4),
+                    rhs_scale=scale_raw[ny][:, f0 : f0 + w],
+                    start=True,
+                    stop=True,
+                )
+
+        def activate(j, which, h):
+            w = WIDTHS[unit(j)[0]]
+            n = 512 // w
+            if (j, which) not in acts:
+                acts[j, which] = work.tile([P, 4, w], F32, name=("th", "sg")[which], bufs=5)
+            nc.scalar.activation(
+                out=acts[j, which][:, n * h : n * (h + 1), :],
+                in_=pbank[j, which, h][:],
+                func=(ACT.Tanh, ACT.Sigmoid)[which],
+                scale=(1.0, 2.0)[which],
+            )
+
+        g01 = keep.tile([P, 8], F32, name="g01")
+        gf = keep.tile([P, 8], F32, name="gf")
+        diag = keep.tile([P, 8, P], BF16, name="diag", align_bytes=64)
+
+        def prepare_gain_v():
+            flat = gain_b[:].rearrange("p g t -> p (g t)")
+            nc.vector.tensor_copy(out=gf[:], in_=flat)
+            nc.vector.tensor_scalar(out=g01[:], in0=flat, scalar1=0.1, scalar2=None, op0=ALU.mult)
+
+        def prepare_diag():
+            for e in range(8):
+                nc.scalar.activation(out=diag[:, e, :], in_=ident[:], func=ACT.Copy, scale=gf[:, e : e + 1])
+
+        gbank, up, wg, wc, ws = {}, {}, {}, {}, {}
+
+        def base(j, b):
+            c, g = unit(j)
+            bank = psum.tile([P, 4, P], F32, name="gb")
+            gbank[j, b] = bank
+            f0 = STARTS[c] + P * b
+            for t in range(4):
+                nc.tensor.matmul(
+                    out=bank[:, t, :], lhsT=diag[:, 4 * g + t, :], rhs=w0t[g][:, t, f0 : f0 + P], start=True, stop=True
+                )
+
+        def hadamard(j):
+            c, g = unit(j)
+            up[j] = work.tile([P, 4, WIDTHS[c]], F32, name="up", bufs=3)
+            for t in range(4):
+                nc.vector.scalar_tensor_tensor(
+                    out=up[j][:, t, :], in0=acts[j, 1][:, t, :], scalar=g01[:, 4 * g + t : 4 * g + t + 1],
+                    in1=acts[j, 0][:, t, :], op0=ALU.mult, op1=ALU.mult,
+                )
+
+        def compose(j, b):
+            w = WIDTHS[unit(j)[0]]
+            if b == 0:
+                wg[j] = work.tile([P, w, 4], BF16, name="wg", align_bytes=64)
+            nc.vector.tensor_tensor(
+                out=wg[j][:, P * b : P * (b + 1), :],
+                in0=up[j][:, :, P * b : P * (b + 1)].rearrange("p t n -> p n t"),
+                in1=gbank[j, b][:].rearrange("p t n -> p n t"),
+                op=ALU.add,
+            )
+
+        def w_quant(j):
+            w = WIDTHS[unit(j)[0]]
+            wc[j] = keep.tile([P, w], I32, name=f"wc{j}", align_bytes=64)
+            ws[j] = keep.tile([P, w], U8, name=f"ws{j}", align_bytes=64)
+            nc.vector.quantize_mx(
+                out=wc[j][:].bitcast(FP8X4), scales=ws[j][:], in_=wg[j][:].rearrange("p n t -> p (n t)")
+            )
+
+        obank, osb = {}, {}
+
+        def apply(c, q):
+            w = WIDTHS[c]
+            n = 512 // w
+            bank = psum.tile([P, n, w], F32, name="ob")
+            obank[c, q] = bank
+            for k in range(n):
+                i = n * q + k
+                for g in range(2):
+                    nc.tensor.matmul_mx(
+                        out=bank[:, k, :],
+                        lhsT=xc[i][:, g, :].bitcast(FP8X4),
+                        lhsT_scale=xsc[i][:, g, :],
+                        rhs=wc[2 * c + g][:].bitcast(FP8X4),
+                        rhs_scale=ws[2 * c + g][:],
+                        start=(g == 0),
+                        stop=(g == 1),
+                    )
+
+        def emit(c, q, on_vector=False):
+            w = WIDTHS[c]
+            n = 512 // w
+            if c not in osb:
+                osb[c] = work.tile([P, NT, w], F32, name="osb", bufs=3)
+            if on_vector:
+                nc.vector.tensor_copy(out=osb[c][:, n * q : n * (q + 1), :], in_=obank[c, q][:])
+            else:
+                nc.scalar.copy(out=osb[c][:, n * q : n * (q + 1), :], in_=obank[c, q][:])
+            if n * (q + 1) % 4 == 0:
+                i0 = n * (q + 1) - 4
+                nc.sync.dma_start(
+                    out=out_v[:, i0 : i0 + 4, STARTS[c] : STARTS[c] + w], in_=osb[c][:, i0 : i0 + 4, :]
+                )
+
+        items = [(j, which, h) for j in range(NU) for which in range(2) for h in range(4 * WIDTHS[j // 2] // 512)]
+        state = {"p": 0, "a": 0}
+
+        def more(n, lead=2):
+            for unused in range(n):
+                while state["p"] < min(len(items), state["a"] + 1 + lead):
+                    product(*items[state["p"]])
+                    state["p"] += 1
+                if state["a"] < len(items):
+                    activate(*items[state["a"]])
+                    state["a"] += 1
+
+        def x_front(i):
+            x_widen(i)
+            x_turn(i)
+
+
+        cells = [(j, b) for j in range(NU) for b in range(WIDTHS[j // 2] // P)]
+        outs = [(c, q) for c in range(NC) for q in range(8 * WIDTHS[c] // 512)]
+        perms = [("s", "x1", 0), ("s", "x1", 1), ("w", "x1", 0), ("s", "x2", 0), ("s", "x2", 1), ("w", "x1", 1), ("w", "x2", 0), ("w", "x2", 1)]
+        for step in ORDER:
+            kind, n = step[0], int(step[1:])
+            if kind == "G":
+                prepare_gain_v()
+            if kind == "D":
+                prepare_diag()
+            if kind == "W":
+                x_widen(n)
+            if kind == "T":
+                x_turn(n)
+            if kind == "O":
+                x_out(n)
+            if kind == "Q":
+                x_quant(n)
+            if kind == "P":
+                (order_scales if perms[n][0] == "s" else order_words)(perms[n][1], perms[n][2])
+            if kind == "M":
+                product(*items[n])
+            if kind == "A":
+                activate(*items[n])
+            if kind == "H":
+                hadamard(n)
+            if kind == "B":
+                base(*cells[n])
+            if kind == "C":
+                compose(*cells[n])
+            if kind == "K":
+                w_quant(n)
+            if kind == "X":
+                apply(*outs[n])
+            if kind == "E":
+                emit(*outs[n])
+            if kind == "V":
+                emit(*outs[n], on_vector=True)

@@ -235,9 +235,9 @@ def tile_fedparatanhhadamardlinear_d1p_kernel(
             if b == 0:
                 wg[j] = work.tile([P, w, 4], BF16, name="wg", align_bytes=64)
             nc.vector.tensor_tensor(
-                out=wg[j][:, P * b : P * (b + 1), :],
-                in0=up[j][:, :, P * b : P * (b + 1)].rearrange("p t n -> p n t"),
-                in1=gbank[j, b][:].rearrange("p t n -> p n t"),
+                out=wg[j][:, P * b : P * (b + 1), :].rearrange("p (c i) t -> p c t i", i=4),
+                in0=up[j][:, :, P * b : P * (b + 1)].rearrange("p t (c i) -> p c t i", i=4),
+                in1=gbank[j, b][:].rearrange("p t (c i) -> p c t i", i=4),
                 op=ALU.add,
             )
 

@@ -23,14 +23,15 @@ NC = len(WIDTHS)
 NU = 2 * NC
 S_WIDEN = (1,)
 ORDER = (
-    "G0 P0 D0 W0 T0 W2 W1 O0 T1 W3 P1 O1 Q0 T2 Q1 O2 T3 O3 W4 Q2 T4 P2 O4 M0 "
-    "W5 A0 P3 P4 T5 P5 O5 M1 Q3 A1 P6 Q4 M2 M3 A2 W6 M4 A3 T6 W7 P7 A4 M5 A5 "
-    "B0 M6 M7 H0 A6 Q5 B1 A7 M8 C0 M9 A8 M10 M11 A9 H1 B2 A10 M12 C1 M13 O6 C2 A11 "
-    "B3 M14 C3 A12 B4 A13 T7 A14 M15 H2 M16 K0 O7 B5 Q6 M17 A15 C4 M18 A16 K1 A17 X0 M19 "
-    "E0 H3 M20 C5 A18 B6 C6 A19 X1 M21 A20 Q7 X2 E1 B7 B8 A21 M22 H4 M23 C7 A22 M24 K2 "
-    "E2 X3 C8 B9 E3 M25 K3 A23 X4 A24 M26 H5 E4 B10 C9 A25 X5 C10 M27 E5 X6 A26 B11 H6 "
-    "C11 M28 A27 M29 K4 B12 A28 K5 B13 C12 E6 X7 A29 M30 H7 X8 E7 M31 A30 H8 C13 X9 E8 B14 "
-    "E9 C14 X10 A31 K6 K7 E10 X11 B15 E11 H9 K8 C15 X12 E12 K9 X13 E13 X14 E14 X15 V15 "
+    "W0 G0 T0 W2 P0 W1 O0 T1 W3 O1 Q0 P1 T2 T3 W4 P2 D0 Q1 O2 M0 O3 M1 W5 Q2 "
+    "A0 T4 Q3 P3 A1 T5 P4 P5 O4 P6 O5 P7 M2 M3 A2 M4 W6 A3 Q4 B0 A4 M5 M6 A5 "
+    "M7 H0 B1 A6 M8 M9 W7 C0 A7 M10 A8 M11 A9 T6 H1 A10 C1 M12 M13 A11 M14 A12 B2 M15 "
+    "H2 A13 B3 C2 M16 A14 M17 K0 A15 C3 M18 O6 B4 M19 A16 T7 H3 A17 C4 M20 A18 M21 Q5 A19 "
+    "B5 K1 B6 C5 O7 X0 Q6 A20 M22 K2 B7 Q7 E0 C6 X1 A21 M23 C7 E1 B8 A22 X2 M24 E2 "
+    "H4 X3 K3 A23 M25 C8 E3 M26 X4 A24 B9 E4 H5 X5 C9 A25 M27 B10 A26 B11 E5 H6 C10 X6 "
+    "A27 M28 C11 M29 E6 B12 K4 A28 X7 K5 B13 A29 M30 H7 C12 E7 X8 A30 C13 X9 E8 K6 B14 E9 "
+    "M31 H8 K7 A31 X10 E10 X11 B15 E11 H9 C14 X12 C15 E12 X13 K8 E13 K9 X14 E14 X15 V15 X16 E16 "
+    "X17 V17 "
 ).split()
 
 
@@ -67,17 +68,17 @@ def tile_fedparatanhhadamardlinear_d1p_kernel(
                 eng.dma_start(out=scale_raw[nm][32 * q : 32 * q + 4, :].bitcast(I32), in_=src[4 * q : 4 * q + 4, :])
 
         xs = keep.tile([P, NT * 8], F32, name="xs")
-        xb = [keep.tile([P, 2, 1024], U8, name=f"xb{h}", align_bytes=64) for h in range(4)]
+        xb = keep.tile([P, NT, 1024], U8, name="xb", align_bytes=64)
         w0t = [keep.tile([P, 4, F], BF16, name=f"w0t{g}", align_bytes=64) for g in range(2)]
-        xraw = {(nm, g): keep.tile([P, 512], I32, name=f"xraw{nm}{g}", align_bytes=64) for nm in ("x1", "x2") for g in range(2)}
+        xraw = {nm: keep.tile([P, 1024], I32, name="xraw" + nm, align_bytes=64) for nm in ("x1", "x2")}
         yw = {nm: keep.tile([P, 1024], I32, name="yw" + nm, align_bytes=64) for nm in ("y1", "y2")}
         gain_b = keep.tile([P, 2, 4], BF16, name="gain_b")
 
-        def load_xb(h):
-            nc.sync.dma_start(out=xb[h][:], in_=x_v[:, 2 * h : 2 * h + 2, :])
+        def load_xb(i0, i1):
+            nc.sync.dma_start(out=xb[:, i0:i1, :], in_=x_v[:, i0:i1, :])
 
-        def load_xw(nm, ap, g, eng=nc.sync):
-            eng.dma_start(out=xraw[nm, g][:], in_=words_of(ap)[:, 512 * g : 512 * (g + 1)])
+        def load_xw(nm, ap, f0, f1, eng=nc.sync):
+            eng.dma_start(out=xraw[nm][:, f0:f1], in_=words_of(ap)[:, f0:f1])
 
         def load_y(nm, ap, f0, f1, eng=nc.sync):
             eng.dma_start(out=yw[nm][:, f0:f1], in_=words_of(ap)[:, f0:f1])
@@ -85,30 +86,32 @@ def tile_fedparatanhhadamardlinear_d1p_kernel(
         def load_w0(g, h):
             nc.sync.dma_start(out=w0t[g][:, :, 512 * h : 512 * (h + 1)], in_=w0_v[g][:, :, 512 * h : 512 * (h + 1)])
 
+        def load_w0_whole(g):
+            nc.gpsimd.dma_start(out=w0t[g][:], in_=w0_v[g])
+
+        make_identity(nc, ident[:])
+        load_scales("y1", y1_scales, nc.gpsimd)
+        load_scales("y2", y2_scales, nc.gpsimd)
+        load_xb(0, 1)
         nc.sync.dma_start(out=gain_b[:], in_=gain.rearrange("(g p t) -> p g t", g=2, t=4))
         nc.sync.dma_start(out=xs[:], in_=x_scale.rearrange("(p i) j -> p (i j)", i=NT))
         load_scales("x1", x1_scales, nc.sync)
-        load_xb(0)
-        load_xb(1)
-        load_scales("y1", y1_scales, nc.sync)
-        load_y("y1", y1_words, 0, 256, nc.sync)
-        load_xb(2)
-        load_xw("x1", x1_words, 0, nc.sync)
-        load_xw("x1", x1_words, 1, nc.sync)
+        load_xb(1, 4)
+        load_xb(4, 8)
+        load_xw("x1", x1_words, 0, 512)
         load_scales("x2", x2_scales, nc.sync)
+        load_y("y1", y1_words, 0, 256, nc.sync)
+        load_xw("x1", x1_words, 512, 1024)
+        load_xw("x2", x2_words, 0, 512)
         load_y("y2", y2_words, 0, 256, nc.sync)
-        load_xw("x2", x2_words, 0, nc.sync)
-        load_xb(3)
-        load_scales("y2", y2_scales, nc.sync)
-        load_xw("x2", x2_words, 1, nc.sync)
+        load_xw("x2", x2_words, 512, 1024)
         load_w0(0, 0)
-        load_y("y1", y1_words, 256, F, nc.sync)
-        load_y("y2", y2_words, 256, F, nc.sync)
+        load_y("y1", y1_words, 256, 1024, nc.sync)
+        load_y("y2", y2_words, 256, 1024, nc.sync)
         load_w0(1, 0)
         load_w0(0, 1)
         load_w0(1, 1)
 
-        make_identity(nc, ident[:])
         nc.scalar.activation(out=warm[:], in_=warm[:], func=ACT.Sigmoid)
 
         xw, xbank, xg, xc, xsc = {}, {}, {}, {}, {}
@@ -117,7 +120,7 @@ def tile_fedparatanhhadamardlinear_d1p_kernel(
             xw[i] = work.tile([P, 1024], BF16, name="xw", align_bytes=64)
             for j in range(8):
                 dst = xw[i][:, 128 * j : 128 * (j + 1)]
-                src = xb[i // 2][:, i % 2, 128 * j : 128 * (j + 1)].bitcast(FP8)
+                src = xb[:, i, 128 * j : 128 * (j + 1)].bitcast(FP8)
                 scale = xs[:, 8 * i + j : 8 * i + j + 1]
                 if i in S_WIDEN:
                     nc.scalar.activation(out=dst, in_=src, func=ACT.Copy, scale=scale)
@@ -151,7 +154,7 @@ def tile_fedparatanhhadamardlinear_d1p_kernel(
 
         def order_words(nm, g):
             xp[nm, g] = keep.tile([P, 4, P], I32, name=f"xp{nm}{g}", align_bytes=64)
-            nc.vector.tensor_copy(out=xp[nm, g][:], in_=xraw[nm, g][:].rearrange("p (m t) -> p t m", t=4))
+            nc.vector.tensor_copy(out=xp[nm, g][:], in_=xraw[nm][:, 512 * g : 512 * (g + 1)].rearrange("p (m t) -> p t m", t=4))
 
         def order_scales(nm, g):
             xps[nm, g] = keep.tile([P, 4, P], U8, name=f"xps{nm}{g}", align_bytes=64)
@@ -170,7 +173,7 @@ def tile_fedparatanhhadamardlinear_d1p_kernel(
             w, f0 = WIDTHS[c], STARTS[c]
             n = 512 // w
             nx, ny = (("x1", "y1"), ("x2", "y2"))[which]
-            bank = psum.tile([P, n, w], F32, name="pb", bufs=4)
+            bank = psum.tile([P, n, w], F32, name="pb", tag="pb", bufs=4)
             pbank[j, which, h] = bank
             for k in range(n):
                 t = n * h + k
@@ -188,7 +191,7 @@ def tile_fedparatanhhadamardlinear_d1p_kernel(
             w = WIDTHS[unit(j)[0]]
             n = 512 // w
             if (j, which) not in acts:
-                acts[j, which] = work.tile([P, 4, w], F32, name=("th", "sg")[which], bufs=5)
+                acts[j, which] = work.tile([P, 4, w], F32, name=("th", "sg")[which], bufs=6)
             nc.scalar.activation(
                 out=acts[j, which][:, n * h : n * (h + 1), :],
                 in_=pbank[j, which, h][:],
@@ -223,7 +226,7 @@ def tile_fedparatanhhadamardlinear_d1p_kernel(
 
         def hadamard(j):
             c, g = unit(j)
-            up[j] = work.tile([P, 4, WIDTHS[c]], F32, name="up", bufs=3)
+            up[j] = work.tile([P, 4, WIDTHS[c]], F32, name="up", bufs=6)
             for t in range(4):
                 nc.vector.scalar_tensor_tensor(
                     out=up[j][:, t, :], in0=acts[j, 1][:, t, :], scalar=g01[:, 4 * g + t : 4 * g + t + 1],
@@ -253,8 +256,11 @@ def tile_fedparatanhhadamardlinear_d1p_kernel(
 
         def apply(c, q):
             w = WIDTHS[c]
-            n = 512 // w
-            bank = psum.tile([P, n, w], F32, name="ob")
+            n = 512 // w if c < NC - 1 else 2
+            if c < NC - 1:
+                bank = psum.tile([P, n, w], F32, name="ob")
+            else:
+                bank = psum.tile([P, n, w], F32, name="lb", tag="pb", bufs=4)
             obank[c, q] = bank
             for k in range(n):
                 i = n * q + k
@@ -271,17 +277,18 @@ def tile_fedparatanhhadamardlinear_d1p_kernel(
 
         def emit(c, q, on_vector=False):
             w = WIDTHS[c]
-            n = 512 // w
+            n = 512 // w if c < NC - 1 else 2
+            m = 4 if c < NC - 1 else 2
             if c not in osb:
                 osb[c] = work.tile([P, NT, w], F32, name="osb", bufs=3)
             if on_vector:
                 nc.vector.tensor_copy(out=osb[c][:, n * q : n * (q + 1), :], in_=obank[c, q][:])
             else:
                 nc.scalar.copy(out=osb[c][:, n * q : n * (q + 1), :], in_=obank[c, q][:])
-            if n * (q + 1) % 4 == 0:
-                i0 = n * (q + 1) - 4
+            if n * (q + 1) % m == 0:
+                i0 = n * (q + 1) - m
                 nc.sync.dma_start(
-                    out=out_v[:, i0 : i0 + 4, STARTS[c] : STARTS[c] + w], in_=osb[c][:, i0 : i0 + 4, :]
+                    out=out_v[:, i0 : i0 + m, STARTS[c] : STARTS[c] + w], in_=osb[c][:, i0 : i0 + m, :]
                 )
 
         items = [(j, which, h) for j in range(NU) for which in range(2) for h in range(4 * WIDTHS[j // 2] // 512)]
@@ -302,7 +309,7 @@ def tile_fedparatanhhadamardlinear_d1p_kernel(
 
 
         cells = [(j, b) for j in range(NU) for b in range(WIDTHS[j // 2] // P)]
-        outs = [(c, q) for c in range(NC) for q in range(8 * WIDTHS[c] // 512)]
+        outs = [(c, q) for c in range(NC) for q in range(8 * WIDTHS[c] // 512 if c < NC - 1 else 4)]
         perms = [("s", "x1", 0), ("s", "x1", 1), ("w", "x1", 0), ("s", "x2", 0), ("s", "x2", 1), ("w", "x1", 1), ("w", "x2", 0), ("w", "x2", 1)]
         for step in ORDER:
             kind, n = step[0], int(step[1:])

@@ -23,14 +23,14 @@ NC = len(WIDTHS)
 NU = 2 * NC
 S_WIDEN = (1,)
 ORDER = (
-    "W0 G0 T0 W2 P0 W1 O0 T1 W3 O1 Q0 P1 T2 T3 W4 P2 D0 Q1 O2 M0 O3 M1 W5 Q2 "
-    "A0 T4 Q3 P3 A1 T5 P4 P5 O4 P6 O5 P7 M2 M3 A2 M4 W6 A3 Q4 B0 A4 M5 M6 A5 "
-    "M7 H0 B1 A6 M8 M9 W7 C0 A7 M10 A8 M11 A9 T6 H1 A10 C1 M12 M13 A11 M14 A12 B2 M15 "
-    "H2 A13 B3 C2 M16 A14 M17 K0 A15 C3 M18 O6 B4 M19 A16 T7 H3 A17 C4 M20 A18 M21 Q5 A19 "
-    "B5 K1 B6 C5 O7 X0 Q6 A20 M22 K2 B7 Q7 E0 C6 X1 A21 M23 C7 E1 B8 A22 X2 M24 E2 "
-    "H4 X3 K3 A23 M25 C8 E3 M26 X4 A24 B9 E4 H5 X5 C9 A25 M27 B10 A26 B11 E5 H6 C10 X6 "
-    "A27 M28 C11 M29 E6 B12 K4 A28 X7 K5 B13 A29 M30 H7 C12 E7 X8 A30 C13 X9 E8 K6 B14 E9 "
-    "M31 H8 K7 A31 X10 E10 X11 B15 E11 H9 C14 X12 C15 E12 X13 K8 E13 K9 X14 E14 X15 V15 X16 E16 "
+    "W0 P0 T0 P1 W1 W2 O0 T1 O1 W3 G0 T2 W4 Q0 T3 Q1 P2 D0 O2 M0 O3 W5 A0 T4 "
+    "W6 Q2 M1 O4 Q3 P3 A1 T5 P4 O5 P5 T6 Q4 O6 P6 M2 Q5 M3 A2 Q6 N0 N1 A3 W7 "
+    "R0 P7 R1 N2 R2 N3 H0 R3 B0 M4 M5 A4 B1 H1 A5 N4 C0 M6 R4 M7 C1 A6 B2 N5 "
+    "C2 A7 N6 B3 K0 R5 T7 R6 M8 N7 H2 A8 C3 B4 R7 N8 M9 C4 O7 M10 B5 K1 A9 B6 "
+    "N9 R8 M11 H3 R9 C5 X0 A10 X1 A11 N10 N11 R10 H4 M12 C6 B7 E0 M13 N12 C7 R11 B8 E1 "
+    "K2 X2 Q7 A12 N13 K3 C8 E2 X3 B9 A13 M14 R12 X4 H5 B10 C9 E3 M15 E4 C10 X5 R13 N14 "
+    "A14 H6 B11 C11 B12 E5 X6 K4 A15 K5 X7 E6 B13 H7 C12 E7 X8 R14 C13 E8 X9 K6 B14 E9 "
+    "N15 H8 K7 R15 X10 E10 X11 B15 E11 H9 C14 X12 C15 E12 X13 K8 E13 K9 X14 E14 X15 V15 X16 E16 "
     "X17 V17 "
 ).split()
 
@@ -90,27 +90,27 @@ def tile_fedparatanhhadamardlinear_d1p_kernel(
             nc.gpsimd.dma_start(out=w0t[g][:], in_=w0_v[g])
 
         make_identity(nc, ident[:])
-        load_scales("y1", y1_scales, nc.gpsimd)
-        load_scales("y2", y2_scales, nc.gpsimd)
         load_xb(0, 1)
-        nc.sync.dma_start(out=gain_b[:], in_=gain.rearrange("(g p t) -> p g t", g=2, t=4))
         nc.sync.dma_start(out=xs[:], in_=x_scale.rearrange("(p i) j -> p (i j)", i=NT))
         load_scales("x1", x1_scales, nc.sync)
         load_xb(1, 4)
         load_xb(4, 8)
         load_xw("x1", x1_words, 0, 512)
-        load_scales("x2", x2_scales, nc.sync)
-        load_y("y1", y1_words, 0, 256, nc.sync)
-        load_xw("x1", x1_words, 512, 1024)
+        nc.sync.dma_start(out=gain_b[:], in_=gain.rearrange("(g p t) -> p g t", g=2, t=4))
         load_xw("x2", x2_words, 0, 512)
+        load_y("y1", y1_words, 0, 256, nc.sync)
+        load_scales("y1", y1_scales, nc.sync)
+        load_scales("x2", x2_scales, nc.sync)
+        load_xw("x1", x1_words, 512, 1024)
+        load_scales("y2", y2_scales, nc.sync)
         load_y("y2", y2_words, 0, 256, nc.sync)
         load_xw("x2", x2_words, 512, 1024)
         load_w0(0, 0)
         load_y("y1", y1_words, 256, 1024, nc.sync)
         load_y("y2", y2_words, 256, 1024, nc.sync)
         load_w0(1, 0)
-        load_w0(0, 1)
         load_w0(1, 1)
+        load_w0(0, 1)
 
         nc.scalar.activation(out=warm[:], in_=warm[:], func=ACT.Sigmoid)
 
@@ -173,7 +173,7 @@ def tile_fedparatanhhadamardlinear_d1p_kernel(
             w, f0 = WIDTHS[c], STARTS[c]
             n = 512 // w
             nx, ny = (("x1", "y1"), ("x2", "y2"))[which]
-            bank = psum.tile([P, n, w], F32, name="pb", tag="pb", bufs=4)
+            bank = psum.tile([P, n, w], F32, name=("pa", "pb")[which], tag=("pa", "pb")[which], bufs=2)
             pbank[j, which, h] = bank
             for k in range(n):
                 t = n * h + k
@@ -191,7 +191,7 @@ def tile_fedparatanhhadamardlinear_d1p_kernel(
             w = WIDTHS[unit(j)[0]]
             n = 512 // w
             if (j, which) not in acts:
-                acts[j, which] = work.tile([P, 4, w], F32, name=("th", "sg")[which], bufs=6)
+                acts[j, which] = work.tile([P, 4, w], F32, name=("th", "sg")[which], bufs=(8, 6)[which])
             nc.scalar.activation(
                 out=acts[j, which][:, n * h : n * (h + 1), :],
                 in_=pbank[j, which, h][:],
@@ -260,7 +260,7 @@ def tile_fedparatanhhadamardlinear_d1p_kernel(
             if c < NC - 1:
                 bank = psum.tile([P, n, w], F32, name="ob")
             else:
-                bank = psum.tile([P, n, w], F32, name="lb", tag="pb", bufs=4)
+                bank = psum.tile([P, n, w], F32, name="lb", tag=("pa", "pb")[q % 2], bufs=2)
             obank[c, q] = bank
             for k in range(n):
                 i = n * q + k
@@ -292,6 +292,8 @@ def tile_fedparatanhhadamardlinear_d1p_kernel(
                 )
 
         items = [(j, which, h) for j in range(NU) for which in range(2) for h in range(4 * WIDTHS[j // 2] // 512)]
+        tanhs = [item for item in items if item[1] == 0]
+        sigmoids = [item for item in items if item[1] == 1]
         state = {"p": 0, "a": 0}
 
         def more(n, lead=2):
@@ -328,9 +330,13 @@ def tile_fedparatanhhadamardlinear_d1p_kernel(
             if kind == "P":
                 (order_scales if perms[n][0] == "s" else order_words)(perms[n][1], perms[n][2])
             if kind == "M":
-                product(*items[n])
+                product(*tanhs[n])
+            if kind == "N":
+                product(*sigmoids[n])
             if kind == "A":
-                activate(*items[n])
+                activate(*tanhs[n])
+            if kind == "R":
+                activate(*sigmoids[n])
             if kind == "H":
                 hadamard(n)
             if kind == "B":

from contextlib import ExitStack

import concourse.mybir as mybir
from concourse.masks import make_identity

T, D, F, R = 1024, 1024, 1024, 512
P = 128
FLOPS = 2 * D * F * R * 2 + 2 * T * D * F

F32 = mybir.dt.float32
BF16 = mybir.dt.bfloat16
I32 = mybir.dt.int32
U8 = mybir.dt.uint8
FP8 = mybir.dt.float8_e4m3fn
FP8X4 = mybir.dt.float8_e4m3fn_x4
ACT = mybir.ActivationFunctionType
ALU = mybir.AluOpType

NT = T // P
WIDTHS = (256, 256, 256, 128, 128)
STARTS = (0, 256, 512, 768, 896)
NC = len(WIDTHS)
NU = 2 * NC
S_WIDEN = (1,)
ORDER = (
    "W0 P0 T0 P1 W1 W2 O0 T1 O1 W3 G0 T2 W4 Q0 T3 Q1 P2 D0 O2 M0 O3 W5 A0 T4 "
    "W6 Q2 M1 O4 Q3 P3 A1 T5 P4 O5 P5 T6 Q4 O6 P6 M2 Q5 M3 A2 Q6 N0 N1 A3 W7 "
    "R0 P7 R1 N2 R2 N3 H0 R3 B0 M4 M5 A4 B1 H1 A5 N4 C0 M6 R4 M7 C1 A6 B2 N5 "
    "C2 A7 N6 B3 K0 R5 T7 R6 M8 N7 H2 A8 C3 B4 R7 N8 M9 C4 O7 M10 B5 K1 A9 B6 "
    "N9 R8 M11 H3 R9 C5 X0 A10 X1 A11 N10 N11 R10 H4 M12 C6 B7 E0 M13 N12 C7 R11 B8 E1 "
    "K2 X2 Q7 A12 N13 K3 C8 E2 X3 B9 A13 M14 R12 X4 H5 B10 C9 E3 M15 E4 C10 X5 R13 N14 "
    "A14 H6 B11 C11 B12 E5 X6 K4 A15 K5 X7 E6 B13 H7 C12 E7 X8 R14 C13 E8 X9 K6 B14 E9 "
    "N15 H8 K7 R15 X10 E10 X11 B15 E11 H9 C14 X12 C15 E12 X13 K8 E13 K9 X14 E14 X15 V15 X16 E16 "
    "X17 V17 "
).split()


def tile_fedparatanhhadamardlinear_d1p_kernel(
    tc, x_bytes, x_scale, w0, x1_words, x1_scales, y1_words, y1_scales,
    x2_words, x2_scales, y2_words, y2_scales, gain, out,
):
    nc = tc.nc
    with ExitStack() as ctx:
        ctx.enter_context(tc.manual_schedule())
        keep = ctx.enter_context(tc.tile_pool(name="keep", bufs=1))
        work = ctx.enter_context(tc.tile_pool(name="work", bufs=3))
        psum = ctx.enter_context(tc.psum_pool(name="psum", bufs=2))

        x_v = x_bytes.rearrange("(p i) k -> p i k", i=NT)
        out_v = out.rearrange("(p i) f -> p i f", i=NT)
        w0_v = w0.rearrange("(g p t) f -> g p t f", g=2, t=4)

        def words_of(ap):
            return ap[0].rearrange("p n t -> p (n t)").bitcast(I32)

        ident = keep.tile([P, P], F32, name="ident", align_bytes=64)
        warm = keep.tile([P, 1], F32, name="warm")
        scale_raw = {}
        for nm in ("x1", "y1", "x2", "y2"):
            scale_raw[nm] = keep.tile([P, 1024], U8, name="sraw_" + nm, align_bytes=64)
        nc.vector.memset(warm[:], 0.0)
        for nm in ("x1", "y1", "x2", "y2"):
            nc.vector.memset(scale_raw[nm][:].bitcast(I32), 0)

        def load_scales(nm, ap, eng):
            src = ap[0].bitcast(I32)
            for q in range(4):
                eng.dma_start(out=scale_raw[nm][32 * q : 32 * q + 4, :].bitcast(I32), in_=src[4 * q : 4 * q + 4, :])

        xs = keep.tile([P, NT * 8], F32, name="xs")
        xb = keep.tile([P, NT, 1024], U8, name="xb", align_bytes=64)
        w0t = [keep.tile([P, 4, F], BF16, name=f"w0t{g}", align_bytes=64) for g in range(2)]
        xraw = {nm: keep.tile([P, 1024], I32, name="xraw" + nm, align_bytes=64) for nm in ("x1", "x2")}
        yw = {nm: keep.tile([P, 1024], I32, name="yw" + nm, align_bytes=64) for nm in ("y1", "y2")}
        gain_b = keep.tile([P, 2, 4], BF16, name="gain_b")

        def load_xb(i0, i1):
            nc.sync.dma_start(out=xb[:, i0:i1, :], in_=x_v[:, i0:i1, :])

        def load_xw(nm, ap, f0, f1, eng=nc.sync):
            eng.dma_start(out=xraw[nm][:, f0:f1], in_=words_of(ap)[:, f0:f1])

        def load_y(nm, ap, f0, f1, eng=nc.sync):
            eng.dma_start(out=yw[nm][:, f0:f1], in_=words_of(ap)[:, f0:f1])

        def load_w0(g, h):
            nc.sync.dma_start(out=w0t[g][:, :, 512 * h : 512 * (h + 1)], in_=w0_v[g][:, :, 512 * h : 512 * (h + 1)])

        def load_w0_whole(g):
            nc.gpsimd.dma_start(out=w0t[g][:], in_=w0_v[g])

        make_identity(nc, ident[:])
        load_xb(0, 1)
        nc.sync.dma_start(out=xs[:], in_=x_scale.rearrange("(p i) j -> p (i j)", i=NT))
        load_scales("x1", x1_scales, nc.sync)
        load_xb(1, 4)
        load_xb(4, 8)
        load_xw("x1", x1_words, 0, 512)
        nc.sync.dma_start(out=gain_b[:], in_=gain.rearrange("(g p t) -> p g t", g=2, t=4))
        load_xw("x2", x2_words, 0, 512)
        load_y("y1", y1_words, 0, 256, nc.sync)
        load_scales("y1", y1_scales, nc.sync)
        load_scales("x2", x2_scales, nc.sync)
        load_xw("x1", x1_words, 512, 1024)
        load_scales("y2", y2_scales, nc.sync)
        load_y("y2", y2_words, 0, 256, nc.sync)
        load_xw("x2", x2_words, 512, 1024)
        load_w0(0, 0)
        load_y("y1", y1_words, 256, 1024, nc.sync)
        load_y("y2", y2_words, 256, 1024, nc.sync)
        load_w0(1, 0)
        load_w0(1, 1)
        load_w0(0, 1)

        nc.scalar.activation(out=warm[:], in_=warm[:], func=ACT.Sigmoid)

        xw, xbank, xg, xc, xsc = {}, {}, {}, {}, {}

        def x_widen(i):
            xw[i] = work.tile([P, 1024], BF16, name="xw", align_bytes=64)
            for j in range(8):
                dst = xw[i][:, 128 * j : 128 * (j + 1)]
                src = xb[:, i, 128 * j : 128 * (j + 1)].bitcast(FP8)
                scale = xs[:, 8 * i + j : 8 * i + j + 1]
                if i in S_WIDEN:
                    nc.scalar.activation(out=dst, in_=src, func=ACT.Copy, scale=scale)
                else:
                    nc.vector.tensor_scalar(out=dst, in0=src, scalar1=scale, scalar2=None, op0=ALU.mult)

        def x_turn(i):
            xbank[i] = psum.tile([P, 4, P], F32, name="ob")
            words = xw[i][:].bitcast(F32)
            for g in range(2):
                for u in range(2):
                    nc.tensor.transpose(xbank[i][:, 2 * g + u, :], words[:, 256 * g + u : 256 * (g + 1) : 2], ident[:])

        def x_out(i):
            xg[i] = work.tile([P, 1024], BF16, name="xg", align_bytes=64)
            nc.scalar.copy(
                out=xg[i][:].bitcast(F32).rearrange("p (g r u) -> p g r u", g=2, u=2),
                in_=xbank[i][:].rearrange("p (g u) r -> p g r u", g=2),
            )

        def x_quant(i):
            xc[i] = keep.tile([P, 2, P], I32, name=f"xc{i}", align_bytes=64)
            xsc[i] = keep.tile([P, 2, P], U8, name=f"xsc{i}", align_bytes=64)
            nc.vector.quantize_mx(
                out=xc[i][:].rearrange("p g r -> p (g r)").bitcast(FP8X4),
                scales=xsc[i][:].rearrange("p g r -> p (g r)"),
                in_=xg[i][:],
            )

        xp, xps = {}, {}

        def order_words(nm, g):
            xp[nm, g] = keep.tile([P, 4, P], I32, name=f"xp{nm}{g}", align_bytes=64)
            nc.vector.tensor_copy(out=xp[nm, g][:], in_=xraw[nm][:, 512 * g : 512 * (g + 1)].rearrange("p (m t) -> p t m", t=4))

        def order_scales(nm, g):
            xps[nm, g] = keep.tile([P, 4, P], U8, name=f"xps{nm}{g}", align_bytes=64)
            nc.vector.tensor_copy(
                out=xps[nm, g][:],
                in_=scale_raw[nm][:, 512 * g : 512 * (g + 1)].rearrange("p (m t) -> p t m", t=4),
            )

        def unit(j):
            return j // 2, j % 2

        acts, pbank = {}, {}

        def product(j, which, h):
            c, g = unit(j)
            w, f0 = WIDTHS[c], STARTS[c]
            n = 512 // w
            nx, ny = (("x1", "y1"), ("x2", "y2"))[which]
            bank = psum.tile([P, n, w], F32, name=("pa", "pb")[which], tag=("pa", "pb")[which], bufs=2)
            pbank[j, which, h] = bank
            for k in range(n):
                t = n * h + k
                nc.tensor.matmul_mx(
                    out=bank[:, k, :],
                    lhsT=xp[nx, g][:, t, :].bitcast(FP8X4),
                    lhsT_scale=xps[nx, g][:, t, :],
                    rhs=yw[ny][:, f0 : f0 + w].bitcast(FP8X4),
                    rhs_scale=scale_raw[ny][:, f0 : f0 + w],
                    start=True,
                    stop=True,
                )

        def activate(j, which, h):
            w = WIDTHS[unit(j)[0]]
            n = 512 // w
            if (j, which) not in acts:
                acts[j, which] = work.tile([P, 4, w], F32, name=("th", "sg")[which], bufs=(8, 6)[which])
            nc.scalar.activation(
                out=acts[j, which][:, n * h : n * (h + 1), :],
                in_=pbank[j, which, h][:],
                func=(ACT.Tanh, ACT.Sigmoid)[which],
                scale=(1.0, 2.0)[which],
            )

        g01 = keep.tile([P, 8], F32, name="g01")
        gf = keep.tile([P, 8], F32, name="gf")
        diag = keep.tile([P, 8, P], BF16, name="diag", align_bytes=64)

        def prepare_gain_v():
            flat = gain_b[:].rearrange("p g t -> p (g t)")
            nc.vector.tensor_copy(out=gf[:], in_=flat)
            nc.vector.tensor_scalar(out=g01[:], in0=flat, scalar1=0.1, scalar2=None, op0=ALU.mult)

        def prepare_diag():
            for e in range(8):
                nc.scalar.activation(out=diag[:, e, :], in_=ident[:], func=ACT.Copy, scale=gf[:, e : e + 1])

        gbank, up, wg, wc, ws = {}, {}, {}, {}, {}

        def base(j, b):
            c, g = unit(j)
            bank = psum.tile([P, 4, P], F32, name="gb")
            gbank[j, b] = bank
            f0 = STARTS[c] + P * b
            for t in range(4):
                nc.tensor.matmul(
                    out=bank[:, t, :], lhsT=diag[:, 4 * g + t, :], rhs=w0t[g][:, t, f0 : f0 + P], start=True, stop=True
                )

        def hadamard(j):
            c, g = unit(j)
            up[j] = work.tile([P, 4, WIDTHS[c]], F32, name="up", bufs=6)
            for t in range(4):
                nc.vector.scalar_tensor_tensor(
                    out=up[j][:, t, :], in0=acts[j, 1][:, t, :], scalar=g01[:, 4 * g + t : 4 * g + t + 1],
                    in1=acts[j, 0][:, t, :], op0=ALU.mult, op1=ALU.mult,
                )

        def compose(j, b):
            w = WIDTHS[unit(j)[0]]
            if b == 0:
                wg[j] = work.tile([P, w, 4], BF16, name="wg", align_bytes=64)
            nc.vector.tensor_tensor(
                out=wg[j][:, P * b : P * (b + 1), :].rearrange("p (c i) t -> p c t i", i=4),
                in0=up[j][:, :, P * b : P * (b + 1)].rearrange("p t (c i) -> p c t i", i=4),
                in1=gbank[j, b][:].rearrange("p t (c i) -> p c t i", i=4),
                op=ALU.add,
            )

        def w_quant(j):
            w = WIDTHS[unit(j)[0]]
            wc[j] = keep.tile([P, w], I32, name=f"wc{j}", align_bytes=64)
            ws[j] = keep.tile([P, w], U8, name=f"ws{j}", align_bytes=64)
            nc.vector.quantize_mx(
                out=wc[j][:].bitcast(FP8X4), scales=ws[j][:], in_=wg[j][:].rearrange("p n t -> p (n t)")
            )

        obank, osb = {}, {}

        def apply(c, q):
            w = WIDTHS[c]
            n = 512 // w if c < NC - 1 else 2
            if c < NC - 1:
                bank = psum.tile([P, n, w], F32, name="ob")
            else:
                bank = psum.tile([P, n, w], F32, name="lb", tag=("pa", "pb")[q % 2], bufs=2)
            obank[c, q] = bank
            for k in range(n):
                i = n * q + k
                for g in range(2):
                    nc.tensor.matmul_mx(
                        out=bank[:, k, :],
                        lhsT=xc[i][:, g, :].bitcast(FP8X4),
                        lhsT_scale=xsc[i][:, g, :],
                        rhs=wc[2 * c + g][:].bitcast(FP8X4),
                        rhs_scale=ws[2 * c + g][:],
                        start=(g == 0),
                        stop=(g == 1),
                    )

        def emit(c, q, on_vector=False):
            w = WIDTHS[c]
            n = 512 // w if c < NC - 1 else 2
            m = 4 if c < NC - 1 else 2
            if c not in osb:
                osb[c] = work.tile([P, NT, w], F32, name="osb", bufs=3)
            if on_vector:
                nc.vector.tensor_copy(out=osb[c][:, n * q : n * (q + 1), :], in_=obank[c, q][:])
            else:
                nc.scalar.copy(out=osb[c][:, n * q : n * (q + 1), :], in_=obank[c, q][:])
            if n * (q + 1) % m == 0:
                i0 = n * (q + 1) - m
                nc.sync.dma_start(
                    out=out_v[:, i0 : i0 + m, STARTS[c] : STARTS[c] + w], in_=osb[c][:, i0 : i0 + m, :]
                )

        items = [(j, which, h) for j in range(NU) for which in range(2) for h in range(4 * WIDTHS[j // 2] // 512)]
        tanhs = [item for item in items if item[1] == 0]
        sigmoids = [item for item in items if item[1] == 1]
        state = {"p": 0, "a": 0}

        def more(n, lead=2):
            for unused in range(n):
                while state["p"] < min(len(items), state["a"] + 1 + lead):
                    product(*items[state["p"]])
                    state["p"] += 1
                if state["a"] < len(items):
                    activate(*items[state["a"]])
                    state["a"] += 1

        def x_front(i):
            x_widen(i)
            x_turn(i)


        cells = [(j, b) for j in range(NU) for b in range(WIDTHS[j // 2] // P)]
        outs = [(c, q) for c in range(NC) for q in range(8 * WIDTHS[c] // 512 if c < NC - 1 else 4)]
        perms = [("s", "x1", 0), ("s", "x1", 1), ("w", "x1", 0), ("s", "x2", 0), ("s", "x2", 1), ("w", "x1", 1), ("w", "x2", 0), ("w", "x2", 1)]
        for step in ORDER:
            kind, n = step[0], int(step[1:])
            if kind == "G":
                prepare_gain_v()
            if kind == "D":
                prepare_diag()
            if kind == "W":
                x_widen(n)
            if kind == "T":
                x_turn(n)
            if kind == "O":
                x_out(n)
            if kind == "Q":
                x_quant(n)
            if kind == "P":
                (order_scales if perms[n][0] == "s" else order_words)(perms[n][1], perms[n][2])
            if kind == "M":
                product(*tanhs[n])
            if kind == "N":
                product(*sigmoids[n])
            if kind == "A":
                activate(*tanhs[n])
            if kind == "R":
                activate(*sigmoids[n])
            if kind == "H":
                hadamard(n)
            if kind == "B":
                base(*cells[n])
            if kind == "C":
                compose(*cells[n])
            if kind == "K":
                w_quant(n)
            if kind == "X":
                apply(*outs[n])
            if kind == "E":
                emit(*outs[n])
            if kind == "V":
                emit(*outs[n], on_vector=True)
